import numpy as np
import ml_dtypes


def mxq(x, axis, fmt="e4m3"):
    dtype, down = {"e4m3": (ml_dtypes.float8_e4m3fn, 7), "e5m2": (ml_dtypes.float8_e5m2, 14)}[fmt]
    v = np.moveaxis(np.asarray(x, np.float32).astype(ml_dtypes.bfloat16).astype(np.float64), axis, -1)
    blocks = v.reshape(v.shape[:-1] + (-1, 32))
    amax = np.abs(blocks).max(-1, keepdims=True)
    byte = np.maximum(np.where(amax > 0, np.frexp(amax)[1] - 1 + 127, 0) - down, 1)
    scale = np.exp2(byte - 127.0)
    codes = (blocks / scale).astype(np.float32).astype(dtype).astype(np.float64)
    return np.moveaxis((codes * scale).reshape(v.shape), -1, axis)


WIDE = False


def mx_kscale(k):
    if not WIDE:
        return np.ones(k)
    levels = np.array([10, -10, 5, -5, 0])
    if k % 512:
        return np.exp2(np.random.permutation(np.resize(levels, k // 32))).repeat(32)
    a = np.empty((k // 512, 16))
    for p in range(k // 512):
        a[p, :8] = np.random.permutation(np.resize(levels, 8))
        for g in range(8):
            far = levels[np.abs(levels - a[p, g]) >= 10]
            a[p, g + 8] = far[np.random.randint(len(far))]
    return np.exp2(a.ravel()).repeat(32)


def f64(x):
    return np.asarray(x).astype(np.float64)


def striped(idx):
    return np.tile(idx.reshape(-1, 16).T, (8, 1)).astype(np.uint16)


def unstriped(offs):
    return offs[:16].T.reshape(-1).astype(np.int64)


def striped8(idx):
    return np.concatenate([x.reshape(-1, 16).T for x in idx]).astype(np.uint16)


def runs(offs, k):
    lists = np.stack([offs[16 * r : 16 * r + 16].T.reshape(-1) for r in range(8)]).astype(np.int64)
    return lists[np.arange(k) % 512 // 64]


def pack_weight(w):
    k, n = w.shape
    w = f64(np.asarray(w, np.float32).astype(ml_dtypes.bfloat16)).reshape(k // 32, 32, n)
    amax = np.abs(w).max(1)
    byte = np.clip(np.where(amax > 0, np.frexp(amax)[1] - 1 + 127 - 7, 1), 1, 254)
    scaled = (w * np.exp2(127.0 - byte)[:, None, :]).reshape(k, n).astype(np.float32)
    words = np.ascontiguousarray(scaled.reshape(k // 512, 128, 4, n).transpose(0, 1, 3, 2)).astype(ml_dtypes.float8_e4m3fn).view(np.uint8)
    return words, np.ascontiguousarray(byte.astype(np.uint8).reshape(k // 512, 16, n))


def unpack_weight(words, scales):
    g, p, n, _ = words.shape
    vals = np.ascontiguousarray(words).view(ml_dtypes.float8_e4m3fn).astype(np.float64) * np.repeat(np.exp2(scales.astype(np.float64) - 127.0), 8, axis=1)[..., None]
    return vals.transpose(0, 1, 3, 2).reshape(g * 512, n)


def sigmoid(v):
    return 1.0 / (1.0 + np.exp(-np.maximum(v, -700.0)))


K, T, S, N, H, C = 512, 2048, 512, 512, 512, 512


def setup_inputs():
    n = np.random.standard_normal
    s = mx_kscale(K)[:, None]
    u = mx_kscale(S)
    packed_xT = pack_weight(n((K, T)) * s)
    return {
        "x_words": packed_xT[0],
        "x_scales": packed_xT[1],
        "w1": (n((K, H)) / np.sqrt(K) / s).astype(np.float32),
        "gs": (np.random.uniform(0.5, 1.5, (K, 1)) / s).astype(np.float32),
        "res": (1.5 * n((N, S))).astype(np.float32),
        "gt": (np.random.uniform(0.5, 1.5, (C, 1)) * u[:, None]).astype(np.float32),
        "w2": (n((C, N)) / np.sqrt(C) / u[:, None]).astype(np.float32),
        "offs": striped(np.random.permutation(T)[:S]),
        "n1": striped8(np.stack([np.random.permutation(S) for _ in range(8)])),
        "cand": striped(np.random.permutation(T)[:C]),
        "n2": striped8(np.stack([np.random.permutation(S) for _ in range(8)])),
    }


def reference(x_words, x_scales, w1, gs, res, gt, w2, offs, n1, cand, n2):
    x_cand = unpack_weight(x_words, x_scales)[:, unstriped(cand)]
    xq = unpack_weight(x_words, x_scales)[:, unstriped(offs)]
    y = mxq(f64(w1), 0, "e4m3").T @ xq
    st = y * (sigmoid(y[np.arange(H)[:, None], runs(n1, H)]))
    z = f64(gs) * (np.maximum(st, st[np.arange(H)[:, None], runs(n1, H)]))
    s = 0.0625 * ((x_cand.T @ mxq(z, 0, "e4m3")))
    z2 = f64(gt) * (np.maximum(s, s[np.arange(C)[:, None], runs(n2, C)]))
    return f64(res) + (mxq(f64(w2), 0, "e4m3").T @ mxq(z2, 0, "e4m3"))

@@ -1,0 +1,174 @@
+from contextlib import ExitStack
+
+import concourse.mybir as mybir
+
+K, T, S = 512, 2048, 512
+P = 128
+PACK = 4
+FLOPS = 3 * 2 * 512 * 512 * 512
+
+F32 = mybir.dt.float32
+BF16 = mybir.dt.bfloat16
+I32 = mybir.dt.int32
+U32 = mybir.dt.uint32
+U16 = mybir.dt.uint16
+U8 = mybir.dt.uint8
+FP8X4 = mybir.dt.float8_e4m3fn_x4
+ALU = mybir.AluOpType
+ACT = mybir.ActivationFunctionType
+
+VECTOR_COLUMNS = 320
+
+
+def tile_picked_readtwicpbig_none_p_kernel(
+    tc, x_words, x_scales, w1, gs, res, gt, w2, offs, n1, cand, n2, out
+):
+    nc = tc.nc
+    with ExitStack() as ctx:
+        keep = ctx.enter_context(tc.tile_pool(name="keep", bufs=1))
+        psum = ctx.enter_context(tc.psum_pool(name="psum", bufs=1))
+
+        def sb(name, shape, dtype):
+            return keep.tile(shape, dtype, name=name, align_bytes=64)
+
+        offs_sb = keep.tile([P, S // 16], U16, name="offs_sb")
+        cand_sb = keep.tile([P, S // 16], U16, name="cand_sb")
+        n1_sb = keep.tile([P, S // 16], U16, name="n1_sb")
+        n2_sb = keep.tile([P, S // 16], U16, name="n2_sb")
+
+        scale_table = sb("scale_table", [P, T], U8)
+        word_table = sb("word_table", [P, T], U32)
+        w1_raw = sb("w1_raw", [P, PACK, S], F32)
+        w2_raw = sb("w2_raw", [P, PACK, S], F32)
+        res_sb = sb("res_sb", [P, PACK, S], F32)
+        gs_sb = sb("gs_sb", [P, PACK], F32)
+        gt_sb = sb("gt_sb", [P, PACK], F32)
+        rows = [sb("rows%d" % t, [P, 2 * S], F32) for t in range(PACK)]
+        gated = [sb("gated%d" % t, [P, 2 * S], F32) for t in range(PACK)]
+
+        nc.vector.memset(scale_table[:].bitcast(I32), 0)
+        for q in range(4):
+            nc.sync.dma_start(
+                out=scale_table[32 * q : 32 * q + 4, :].bitcast(I32),
+                in_=x_scales[0, 4 * q : 4 * q + 4, :].bitcast(I32),
+            )
+        nc.sync.dma_start(offs_sb[:], offs)
+        nc.sync.dma_start(out=w1_raw[:], in_=w1.rearrange("(p j) c -> p j c", j=PACK))
+        nc.sync.dma_start(out=word_table[:].bitcast(I32), in_=x_words[0].rearrange("p c r -> p (c r)").bitcast(I32))
+        nc.sync.dma_start(cand_sb[:], cand)
+        nc.sync.dma_start(n1_sb[:], n1)
+        nc.sync.dma_start(out=gs_sb[:], in_=gs.rearrange("(p t) o -> p (t o)", t=PACK))
+        nc.sync.dma_start(out=w2_raw[:], in_=w2.rearrange("(p j) c -> p j c", j=PACK))
+        nc.sync.dma_start(n2_sb[:], n2)
+        nc.sync.dma_start(out=gt_sb[:], in_=gt.rearrange("(p t) o -> p (t o)", t=PACK))
+        nc.sync.dma_start(out=res_sb[:], in_=res.rearrange("(t p) c -> p t c", p=P))
+        for t in range(PACK):
+            nc.vector.memset(rows[t][:, S:], 0.0)
+
+        warm = sb("warm", [P, 1], F32)
+        nc.scalar.activation(warm[:], rows[0][:, S : S + 1], ACT.Sigmoid)
+
+        def quantize(name, grouped):
+            codes = sb(name + "_codes", [P, S], U32)
+            scales = sb(name + "_scales", [P, S], U8)
+            nc.vector.quantize_mx(out=codes[:].bitcast(FP8X4), scales=scales[:], in_=grouped[:])
+            return codes, scales
+
+        def product(acc, lhs, rhs, t):
+            cols = slice(t * P, (t + 1) * P)
+            nc.tensor.matmul_mx(
+                out=acc[:],
+                lhsT=lhs[0][:, cols].bitcast(FP8X4),
+                lhsT_scale=lhs[1][:, cols],
+                rhs=rhs[0][:].bitcast(FP8X4),
+                rhs_scale=rhs[1][:],
+                start=True,
+                stop=True,
+            )
+
+        def interleave(grouped, planes):
+            dst = grouped[:].rearrange("p (c i t) -> p c t i", i=4, t=PACK)
+            src = planes[:].rearrange("p t (c i) -> p c t i", i=4)
+            cut = VECTOR_COLUMNS // 4
+            nc.vector.tensor_copy(out=dst[:, :cut], in_=src[:, :cut])
+            nc.scalar.copy(out=dst[:, cut:], in_=src[:, cut:])
+
+        xq_scales = sb("xq_scales", [P, S], U8)
+        xq_words = sb("xq_words", [P, S], U32)
+        xc_scales_listed = sb("xc_scales_listed", [P, S], U8)
+        xc_words_listed = sb("xc_words_listed", [P, S], U32)
+        xc_scales = sb("xc_scales", [P, S], U8)
+        xc_words = sb("xc_words", [P, S], U32)
+        nc.vector.tensor_copy(xq_scales[:], scale_table[:].indirect(offs_sb[:]))
+        nc.vector.tensor_copy(xc_scales_listed[:], scale_table[:].indirect(cand_sb[:]))
+
+        w1_grouped = sb("w1_grouped", [P, PACK * S], BF16)
+        nc.scalar.copy(
+            out=w1_grouped[:].rearrange("p (t m j) -> p m j t", t=PACK, j=PACK),
+            in_=w1_raw[:].rearrange("p j (m t) -> p m j t", t=PACK),
+        )
+        w1_q = quantize("w1", w1_grouped)
+        nc.vector.tensor_copy(xq_words[:], word_table[:].indirect(offs_sb[:]))
+        nc.vector.tensor_copy(xc_words_listed[:], word_table[:].indirect(cand_sb[:]))
+        nc.vector.tensor_copy(
+            out=xc_words[:].rearrange("p (t m) -> p m t", t=PACK),
+            in_=xc_words_listed[:].rearrange("p (m t) -> p m t", t=PACK),
+        )
+        nc.vector.tensor_copy(
+            out=xc_scales[:].rearrange("p (t m) -> p m t", t=PACK),
+            in_=xc_scales_listed[:].rearrange("p (m t) -> p m t", t=PACK),
+        )
+
+        fetched = [sb("fetched%d" % t, [P, S], F32) for t in range(2)]
+        larger = [sb("larger%d" % t, [P, S], F32) for t in range(PACK)]
+
+        def weigh(planes, t, weight):
+            if t < PACK - 1:
+                nc.scalar.activation(planes[:, t, :], larger[t][:], ACT.Copy, scale=weight[:, t : t + 1])
+            else:
+                nc.vector.tensor_scalar(planes[:, t, :], larger[t][:], weight[:, t : t + 1], None, ALU.mult)
+
+        z_planes = sb("z_planes", [P, PACK, S], BF16)
+        ys = []
+        for t in range(PACK):
+            y = psum.tile([P, S], F32, name="first%d" % t, tag="first%d" % t)
+            product(y, w1_q, (xq_words, xq_scales), t)
+            ys.append(y)
+        for t in range(PACK):
+            nc.scalar.copy(rows[t][:, :S], ys[t][:])
+            nc.scalar.activation(gated[t][:, S:], rows[t][:].indirect(n1_sb[:]), ACT.Sigmoid)
+        for t in range(PACK):
+            nc.vector.tensor_tensor(gated[t][:, :S], ys[t][:], gated[t][:, S:], ALU.mult)
+            nc.vector.tensor_copy(fetched[t % 2][:], gated[t][:].indirect(n1_sb[:]))
+            nc.vector.tensor_tensor(larger[t][:], gated[t][:, :S], fetched[t % 2][:], ALU.max)
+            weigh(z_planes, t, gs_sb)
+        z_grouped = sb("z_grouped", [P, PACK * S], BF16)
+        interleave(z_grouped, z_planes)
+        z_q = quantize("z", z_grouped)
+
+        w2_grouped = sb("w2_grouped", [P, PACK * S], BF16)
+        nc.scalar.copy(
+            out=w2_grouped[:].rearrange("p (c i j) -> p c j i", i=4, j=PACK),
+            in_=w2_raw[:].rearrange("p j (c i) -> p c j i", i=4),
+        )
+        w2_q = quantize("w2", w2_grouped)
+
+        z2_planes = sb("z2_planes", [P, PACK, S], BF16)
+        for t in range(PACK):
+            s = psum.tile([P, S], F32, name="second%d" % t, tag="second%d" % t)
+            product(s, (xc_words, xc_scales), z_q, t)
+            nc.scalar.activation(rows[t][:, :S], s[:], ACT.Copy, scale=0.0625)
+        for t in range(PACK):
+            nc.vector.tensor_copy(fetched[t % 2][:], rows[t][:].indirect(n2_sb[:]))
+            nc.vector.tensor_tensor(larger[t][:], rows[t][:, :S], fetched[t % 2][:], ALU.max)
+            weigh(z2_planes, t, gt_sb)
+        z2_grouped = sb("z2_grouped", [P, PACK * S], BF16)
+        interleave(z2_grouped, z2_planes)
+        z2_q = quantize("z2", z2_grouped)
+
+        result = sb("result", [P, PACK, S], F32)
+        for t in range(PACK):
+            o = psum.tile([P, S], F32, name="third%d" % t, tag="first%d" % t)
+            product(o, w2_q, z2_q, t)
+            nc.vector.tensor_tensor(result[:, t, :], o[:], res_sb[:, t, :], ALU.add)
+            nc.sync.dma_start(out=out[t * P : (t + 1) * P, :], in_=result[:, t, :])

@@ -5,6 +5,7 @@ import concourse.mybir as mybir
 K, T, S = 512, 2048, 512
 P = 128
 PACK = 4
+HALF = S // 2
 FLOPS = 3 * 2 * 512 * 512 * 512
 
 F32 = mybir.dt.float32
@@ -17,8 +18,6 @@ FP8X4 = mybir.dt.float8_e4m3fn_x4
 ALU = mybir.AluOpType
 ACT = mybir.ActivationFunctionType
 
-VECTOR_COLUMNS = 320
-
 
 def tile_picked_readtwicpbig_none_p_kernel(
     tc, x_words, x_scales, w1, gs, res, gt, w2, offs, n1, cand, n2, out
@@ -28,8 +27,14 @@ def tile_picked_readtwicpbig_none_p_kernel(
         keep = ctx.enter_context(tc.tile_pool(name="keep", bufs=1))
         psum = ctx.enter_context(tc.psum_pool(name="psum", bufs=1))
 
-        def sb(name, shape, dtype):
-            return keep.tile(shape, dtype, name=name, align_bytes=64)
+        def sb(name, shape, dtype, tag=None):
+            return keep.tile(shape, dtype, name=name, tag=tag or name, align_bytes=64)
+
+        def bank(name, number, shape):
+            return psum.tile(shape, F32, name=name, tag="bank%d" % number)
+
+        halves = [slice(h * HALF, (h + 1) * HALF) for h in range(2)]
+        list_halves = [slice(h * HALF // 16, (h + 1) * HALF // 16) for h in range(2)]
 
         offs_sb = keep.tile([P, S // 16], U16, name="offs_sb")
         cand_sb = keep.tile([P, S // 16], U16, name="cand_sb")
@@ -38,88 +43,108 @@ def tile_picked_readtwicpbig_none_p_kernel(
 
         scale_table = sb("scale_table", [P, T], U8)
         word_table = sb("word_table", [P, T], U32)
-        w1_raw = sb("w1_raw", [P, PACK, S], F32)
-        w2_raw = sb("w2_raw", [P, PACK, S], F32)
-        res_sb = sb("res_sb", [P, PACK, S], F32)
+        w1_raw = [sb("w1_raw%d" % h, [P, PACK, HALF], F32, tag="weights%d" % h) for h in range(2)]
         gs_sb = sb("gs_sb", [P, PACK], F32)
         gt_sb = sb("gt_sb", [P, PACK], F32)
-        rows = [sb("rows%d" % t, [P, 2 * S], F32) for t in range(PACK)]
+        y_rows = [sb("y_row%d" % u, [P, 2 * S], F32) for u in range(2)]
         gated = [sb("gated%d" % t, [P, 2 * S], F32) for t in range(PACK)]
 
-        nc.vector.memset(scale_table[:].bitcast(I32), 0)
+        scale_rows = sb("scale_rows", [P, T // 4], I32)
         for q in range(4):
             nc.sync.dma_start(
-                out=scale_table[32 * q : 32 * q + 4, :].bitcast(I32),
-                in_=x_scales[0, 4 * q : 4 * q + 4, :].bitcast(I32),
+                out=scale_rows[32 * q : 32 * q + 4, :], in_=x_scales[0, 4 * q : 4 * q + 4, :].bitcast(I32)
             )
         nc.sync.dma_start(offs_sb[:], offs)
-        nc.sync.dma_start(out=w1_raw[:], in_=w1.rearrange("(p j) c -> p j c", j=PACK))
-        nc.sync.dma_start(out=word_table[:].bitcast(I32), in_=x_words[0].rearrange("p c r -> p (c r)").bitcast(I32))
         nc.sync.dma_start(cand_sb[:], cand)
+        for h in range(2):
+            nc.sync.dma_start(out=w1_raw[h][:], in_=w1.rearrange("(p j) c -> p j c", j=PACK)[:, :, halves[h]])
+        nc.sync.dma_start(out=word_table[:].bitcast(I32), in_=x_words[0].rearrange("p c r -> p (c r)").bitcast(I32))
         nc.sync.dma_start(n1_sb[:], n1)
         nc.sync.dma_start(out=gs_sb[:], in_=gs.rearrange("(p t) o -> p (t o)", t=PACK))
-        nc.sync.dma_start(out=w2_raw[:], in_=w2.rearrange("(p j) c -> p j c", j=PACK))
         nc.sync.dma_start(n2_sb[:], n2)
         nc.sync.dma_start(out=gt_sb[:], in_=gt.rearrange("(p t) o -> p (t o)", t=PACK))
-        nc.sync.dma_start(out=res_sb[:], in_=res.rearrange("(t p) c -> p t c", p=P))
-        for t in range(PACK):
-            nc.vector.memset(rows[t][:, S:], 0.0)
+        nc.vector.memset(scale_table[:].bitcast(I32), 0)
+        for u in range(2):
+            nc.vector.memset(y_rows[u][:, S:].bitcast(I32), 0)
 
         warm = sb("warm", [P, 1], F32)
-        nc.scalar.activation(warm[:], rows[0][:, S : S + 1], ACT.Sigmoid)
+        nc.scalar.activation(warm[:], y_rows[0][:, S : S + 1], ACT.Sigmoid)
 
-        def quantize(name, grouped):
-            codes = sb(name + "_codes", [P, S], U32)
-            scales = sb(name + "_scales", [P, S], U8)
-            nc.vector.quantize_mx(out=codes[:].bitcast(FP8X4), scales=scales[:], in_=grouped[:])
-            return codes, scales
-
-        def product(acc, lhs, rhs, t):
-            cols = slice(t * P, (t + 1) * P)
+        def product(acc, lhs, rhs, t, cols):
+            lhs_cols = slice(t * P, (t + 1) * P)
             nc.tensor.matmul_mx(
-                out=acc[:],
-                lhsT=lhs[0][:, cols].bitcast(FP8X4),
-                lhsT_scale=lhs[1][:, cols],
-                rhs=rhs[0][:].bitcast(FP8X4),
-                rhs_scale=rhs[1][:],
+                out=acc,
+                lhsT=lhs[0][:, lhs_cols].bitcast(FP8X4),
+                lhsT_scale=lhs[1][:, lhs_cols],
+                rhs=rhs[0][:, cols].bitcast(FP8X4),
+                rhs_scale=rhs[1][:, cols],
                 start=True,
                 stop=True,
             )
 
-        def interleave(grouped, planes):
-            dst = grouped[:].rearrange("p (c i t) -> p c t i", i=4, t=PACK)
-            src = planes[:].rearrange("p t (c i) -> p c t i", i=4)
-            cut = VECTOR_COLUMNS // 4
-            nc.vector.tensor_copy(out=dst[:, :cut], in_=src[:, :cut])
-            nc.scalar.copy(out=dst[:, cut:], in_=src[:, cut:])
+        def interleave_and_quantize(name, planes):
+            codes = sb(name + "_codes", [P, S], U32)
+            scales = sb(name + "_scales", [P, S], U8)
+            grouped = [sb("%s_grouped%d" % (name, h), [P, PACK * HALF], BF16) for h in range(2)]
 
+            def interleave(copy, h, lo, hi):
+                copy(
+                    grouped[h][:, PACK * lo : PACK * hi].rearrange("p (c i t) -> p c t i", i=4, t=PACK),
+                    planes[:, :, h * HALF + lo : h * HALF + hi].rearrange("p t (c i) -> p c t i", i=4),
+                )
+
+            def quantize(h):
+                nc.vector.quantize_mx(
+                    out=codes[:, halves[h]].bitcast(FP8X4), scales=scales[:, halves[h]], in_=grouped[h][:]
+                )
+
+            interleave(nc.scalar.copy, 1, HALF // 2, HALF)
+            interleave(nc.vector.tensor_copy, 0, 0, HALF)
+            interleave(nc.vector.tensor_copy, 1, 0, HALF // 2)
+            quantize(0)
+            quantize(1)
+            return codes, scales
+
+        for q in range(4):
+            nc.vector.tensor_copy(scale_table[32 * q : 32 * q + 4, :].bitcast(I32), scale_rows[32 * q : 32 * q + 4, :])
         xq_scales = sb("xq_scales", [P, S], U8)
-        xq_words = sb("xq_words", [P, S], U32)
         xc_scales_listed = sb("xc_scales_listed", [P, S], U8)
-        xc_words_listed = sb("xc_words_listed", [P, S], U32)
         xc_scales = sb("xc_scales", [P, S], U8)
-        xc_words = sb("xc_words", [P, S], U32)
         nc.vector.tensor_copy(xq_scales[:], scale_table[:].indirect(offs_sb[:]))
         nc.vector.tensor_copy(xc_scales_listed[:], scale_table[:].indirect(cand_sb[:]))
-
-        w1_grouped = sb("w1_grouped", [P, PACK * S], BF16)
-        nc.scalar.copy(
-            out=w1_grouped[:].rearrange("p (t m j) -> p m j t", t=PACK, j=PACK),
-            in_=w1_raw[:].rearrange("p j (m t) -> p m j t", t=PACK),
+        nc.vector.tensor_copy(
+            out=xc_scales[:].rearrange("p (t c i) -> p c t i", t=PACK, i=16),
+            in_=xc_scales_listed[:].rearrange("p (c i t) -> p c t i", t=PACK, i=16),
         )
-        w1_q = quantize("w1", w1_grouped)
-        nc.vector.tensor_copy(xq_words[:], word_table[:].indirect(offs_sb[:]))
+
+        w1_grouped = sb("w1_grouped", [P, PACK * S], BF16, tag="residual")
+        for h in range(2):
+            nc.scalar.copy(
+                out=w1_grouped[:].rearrange("p (t m j) -> p m j t", t=PACK, j=PACK)[:, h * P // 2 : (h + 1) * P // 2],
+                in_=w1_raw[h][:].rearrange("p j (m t) -> p m j t", t=PACK),
+            )
+        w1_codes = sb("w1_codes", [P, S], U32)
+        w1_scales = sb("w1_scales", [P, S], U8, tag="xc_scales_listed")
+        nc.vector.quantize_mx(out=w1_codes[:].bitcast(FP8X4), scales=w1_scales[:], in_=w1_grouped[:])
+
+        xq_words = sb("xq_words", [P, S], U32, tag="scale_table")
+        xc_words_listed = sb("xc_words_listed", [P, S], U32)
+        xc_words = sb("xc_words", [P, S], U32)
+        for h in range(2):
+            nc.vector.tensor_copy(xq_words[:, halves[h]], word_table[:].indirect(offs_sb[:, list_halves[h]]))
         nc.vector.tensor_copy(xc_words_listed[:], word_table[:].indirect(cand_sb[:]))
         nc.vector.tensor_copy(
-            out=xc_words[:].rearrange("p (t m) -> p m t", t=PACK),
-            in_=xc_words_listed[:].rearrange("p (m t) -> p m t", t=PACK),
-        )
-        nc.vector.tensor_copy(
-            out=xc_scales[:].rearrange("p (t m) -> p m t", t=PACK),
-            in_=xc_scales_listed[:].rearrange("p (m t) -> p m t", t=PACK),
+            out=xc_words[:].rearrange("p (t c i) -> p c t i", t=PACK, i=4),
+            in_=xc_words_listed[:].rearrange("p (c i t) -> p c t i", t=PACK, i=4),
         )
 
-        fetched = [sb("fetched%d" % t, [P, S], F32) for t in range(2)]
+        w2_raw = [sb("w2_raw%d" % h, [P, PACK, HALF], F32, tag="weights%d" % h) for h in range(2)]
+        res_sb = sb("res_sb", [P, PACK, S], F32, tag="residual")
+        for h in range(2):
+            nc.sync.dma_start(out=w2_raw[h][:], in_=w2.rearrange("(p j) c -> p j c", j=PACK)[:, :, halves[h]])
+        nc.sync.dma_start(out=res_sb[:], in_=res.rearrange("(t p) c -> p t c", p=P))
+
+        fetched = [sb("fetched%d" % t, [P, S], F32) for t in range(PACK)]
         larger = [sb("larger%d" % t, [P, S], F32) for t in range(PACK)]
 
         def weigh(planes, t, weight):
@@ -128,47 +153,70 @@ def tile_picked_readtwicpbig_none_p_kernel(
             else:
                 nc.vector.tensor_scalar(planes[:, t, :], larger[t][:], weight[:, t : t + 1], None, ALU.mult)
 
-        z_planes = sb("z_planes", [P, PACK, S], BF16)
-        ys = []
-        for t in range(PACK):
-            y = psum.tile([P, S], F32, name="first%d" % t, tag="first%d" % t)
-            product(y, w1_q, (xq_words, xq_scales), t)
-            ys.append(y)
-        for t in range(PACK):
-            nc.scalar.copy(rows[t][:, :S], ys[t][:])
-            nc.scalar.activation(gated[t][:, S:], rows[t][:].indirect(n1_sb[:]), ACT.Sigmoid)
-        for t in range(PACK):
-            nc.vector.tensor_tensor(gated[t][:, :S], ys[t][:], gated[t][:, S:], ALU.mult)
-            nc.vector.tensor_copy(fetched[t % 2][:], gated[t][:].indirect(n1_sb[:]))
-            nc.vector.tensor_tensor(larger[t][:], gated[t][:, :S], fetched[t % 2][:], ALU.max)
-            weigh(z_planes, t, gs_sb)
-        z_grouped = sb("z_grouped", [P, PACK * S], BF16)
-        interleave(z_grouped, z_planes)
-        z_q = quantize("z", z_grouped)
+        def row_products(name, lhs, rhs):
+            pieces = []
+            for t in range(PACK):
+                for cols in halves if t == 0 else [slice(0, S)]:
+                    acc = bank("%s%d" % (name, len(pieces)), len(pieces), [P, cols.stop - cols.start])
+                    product(acc[:], lhs, rhs, t, cols)
+                    pieces.append((t, cols, acc))
+            return pieces
 
-        w2_grouped = sb("w2_grouped", [P, PACK * S], BF16)
-        nc.scalar.copy(
-            out=w2_grouped[:].rearrange("p (c i j) -> p c j i", i=4, j=PACK),
-            in_=w2_raw[:].rearrange("p j (c i) -> p c j i", i=4),
-        )
-        w2_q = quantize("w2", w2_grouped)
+        def shifted(cols):
+            return slice(cols.start + S, cols.stop + S)
+
+        def listed(cols):
+            return slice(cols.start // 16, cols.stop // 16)
+
+        z_planes = sb("z_planes", [P, PACK, S], BF16)
+        y_pieces = row_products("y", (w1_codes, w1_scales), (xq_words, xq_scales))
+        for t in range(PACK):
+            for row, cols, acc in [piece for piece in y_pieces if piece[0] == t]:
+                nc.scalar.copy(y_rows[t % 2][:, cols], acc[:])
+            for row, cols, acc in [piece for piece in y_pieces if piece[0] == t]:
+                nc.scalar.activation(gated[t][:, shifted(cols)], y_rows[t % 2][:].indirect(n1_sb[:, listed(cols)]), ACT.Sigmoid)
+
+        def gate(t):
+            for row, cols, acc in [piece for piece in y_pieces if piece[0] == t]:
+                nc.vector.tensor_tensor(gated[t][:, cols], acc[:], gated[t][:, shifted(cols)], ALU.mult)
+
+        gate(0)
+        for t in range(PACK):
+            nc.vector.tensor_copy(fetched[t][:], gated[t][:].indirect(n1_sb[:]))
+            if t + 1 < PACK:
+                gate(t + 1)
+            nc.vector.tensor_tensor(larger[t][:], gated[t][:, :S], fetched[t][:], ALU.max)
+            weigh(z_planes, t, gs_sb)
+        z_q = interleave_and_quantize("z", z_planes)
+
+        w2_grouped = sb("w2_grouped", [P, PACK * S], BF16, tag="y_row1")
+        for h in range(2):
+            nc.scalar.copy(
+                out=w2_grouped[:, h * PACK * HALF : (h + 1) * PACK * HALF].rearrange("p (c i j) -> p c j i", i=4, j=PACK),
+                in_=w2_raw[h][:].rearrange("p j (c i) -> p c j i", i=4),
+            )
+        w2_codes = sb("w2_codes", [P, S], U32, tag="z_grouped1")
+        w2_scales = sb("w2_scales", [P, S], U8)
+        nc.vector.quantize_mx(out=w2_codes[:].bitcast(FP8X4), scales=w2_scales[:], in_=w2_grouped[:])
 
         z2_planes = sb("z2_planes", [P, PACK, S], BF16)
+        for t, cols, acc in row_products("s", (xc_words, xc_scales), z_q):
+            nc.scalar.activation(gated[t][:, cols], acc[:], ACT.Copy, scale=0.0625)
+        nc.vector.tensor_copy(fetched[0][:], gated[0][:].indirect(n2_sb[:]))
         for t in range(PACK):
-            s = psum.tile([P, S], F32, name="second%d" % t, tag="second%d" % t)
-            product(s, (xc_words, xc_scales), z_q, t)
-            nc.scalar.activation(rows[t][:, :S], s[:], ACT.Copy, scale=0.0625)
-        for t in range(PACK):
-            nc.vector.tensor_copy(fetched[t % 2][:], rows[t][:].indirect(n2_sb[:]))
-            nc.vector.tensor_tensor(larger[t][:], rows[t][:, :S], fetched[t % 2][:], ALU.max)
+            if t + 1 < PACK:
+                nc.vector.tensor_copy(fetched[t + 1][:], gated[t + 1][:].indirect(n2_sb[:]))
+            nc.vector.tensor_tensor(larger[t][:], gated[t][:, :S], fetched[t][:], ALU.max)
             weigh(z2_planes, t, gt_sb)
-        z2_grouped = sb("z2_grouped", [P, PACK * S], BF16)
-        interleave(z2_grouped, z2_planes)
-        z2_q = quantize("z2", z2_grouped)
+        z2_q = interleave_and_quantize("z2", z2_planes)
 
-        result = sb("result", [P, PACK, S], F32)
-        for t in range(PACK):
-            o = psum.tile([P, S], F32, name="third%d" % t, tag="first%d" % t)
-            product(o, w2_q, z2_q, t)
-            nc.vector.tensor_tensor(result[:, t, :], o[:], res_sb[:, t, :], ALU.add)
-            nc.sync.dma_start(out=out[t * P : (t + 1) * P, :], in_=result[:, t, :])
+        out_rows = out.rearrange("(t p) c -> p t c", p=P)
+        for h in range(2):
+            for pair in range(2):
+                acc = bank("o%d%d" % (h, pair), 2 * h + pair, [P, 2, HALF])
+                for u in range(2):
+                    product(acc[:, u, :], (w2_codes, w2_scales), z2_q, 2 * pair + u, halves[h])
+                tiles = slice(2 * pair, 2 * pair + 2)
+                result = sb("result%d%d" % (h, pair), [P, 2, HALF], F32)
+                nc.vector.tensor_tensor(result[:], acc[:], res_sb[:, tiles, halves[h]], ALU.add)
+                nc.sync.dma_start(out=out_rows[:, tiles, halves[h]], in_=result[:])

@@ -34,6 +34,7 @@ def tile_picked_readtwicpbig_none_p_kernel(
             return psum.tile(shape, F32, name=name, tag="bank%d" % number)
 
         halves = [slice(h * HALF, (h + 1) * HALF) for h in range(2)]
+        thirds = [halves[0], slice(HALF, HALF + P), slice(HALF + P, S)]
         list_halves = [slice(h * HALF // 16, (h + 1) * HALF // 16) for h in range(2)]
 
         offs_sb = keep.tile([P, S // 16], U16, name="offs_sb")
@@ -43,7 +44,7 @@ def tile_picked_readtwicpbig_none_p_kernel(
 
         scale_table = sb("scale_table", [P, T], U8)
         word_table = sb("word_table", [P, T], U32)
-        w1_raw = [sb("w1_raw%d" % h, [P, PACK, HALF], F32, tag="weights%d" % h) for h in range(2)]
+        w1_raw = sb("w1_raw", [P, PACK, S], F32, tag="weights")
         gs_sb = sb("gs_sb", [P, PACK], F32)
         gt_sb = sb("gt_sb", [P, PACK], F32)
         y_rows = [sb("y_row%d" % u, [P, 2 * S], F32) for u in range(2)]
@@ -55,10 +56,9 @@ def tile_picked_readtwicpbig_none_p_kernel(
                 out=scale_rows[32 * q : 32 * q + 4, :], in_=x_scales[0, 4 * q : 4 * q + 4, :].bitcast(I32)
             )
         nc.sync.dma_start(offs_sb[:], offs)
-        nc.sync.dma_start(cand_sb[:], cand)
-        for h in range(2):
-            nc.sync.dma_start(out=w1_raw[h][:], in_=w1.rearrange("(p j) c -> p j c", j=PACK)[:, :, halves[h]])
+        nc.sync.dma_start(out=w1_raw[:], in_=w1.rearrange("(p j) c -> p j c", j=PACK))
         nc.sync.dma_start(out=word_table[:].bitcast(I32), in_=x_words[0].rearrange("p c r -> p (c r)").bitcast(I32))
+        nc.sync.dma_start(cand_sb[:], cand)
         nc.sync.dma_start(n1_sb[:], n1)
         nc.sync.dma_start(out=gs_sb[:], in_=gs.rearrange("(p t) o -> p (t o)", t=PACK))
         nc.sync.dma_start(n2_sb[:], n2)
@@ -66,6 +66,7 @@ def tile_picked_readtwicpbig_none_p_kernel(
         nc.vector.memset(scale_table[:].bitcast(I32), 0)
         for u in range(2):
             nc.vector.memset(y_rows[u][:, S:].bitcast(I32), 0)
+
 
         warm = sb("warm", [P, 1], F32)
         nc.scalar.activation(warm[:], y_rows[0][:, S : S + 1], ACT.Sigmoid)
@@ -82,52 +83,39 @@ def tile_picked_readtwicpbig_none_p_kernel(
                 stop=True,
             )
 
-        def interleave_and_quantize(name, planes):
+        def interleave_and_quantize(name, planes, tags):
             codes = sb(name + "_codes", [P, S], U32)
             scales = sb(name + "_scales", [P, S], U8)
-            grouped = [sb("%s_grouped%d" % (name, h), [P, PACK * HALF], BF16) for h in range(2)]
-
-            def interleave(copy, h, lo, hi):
+            grouped = [
+                sb("%s_grouped%d" % (name, n), [P, PACK * (cols.stop - cols.start)], BF16, tag=tags[n])
+                for n, cols in enumerate(thirds)
+            ]
+            for n, copy in enumerate((nc.vector.tensor_copy, nc.vector.tensor_copy, nc.scalar.copy)):
                 copy(
-                    grouped[h][:, PACK * lo : PACK * hi].rearrange("p (c i t) -> p c t i", i=4, t=PACK),
-                    planes[:, :, h * HALF + lo : h * HALF + hi].rearrange("p t (c i) -> p c t i", i=4),
+                    grouped[n][:].rearrange("p (c i t) -> p c t i", i=4, t=PACK),
+                    planes[:, :, thirds[n]].rearrange("p t (c i) -> p c t i", i=4),
                 )
-
-            def quantize(h):
-                nc.vector.quantize_mx(
-                    out=codes[:, halves[h]].bitcast(FP8X4), scales=scales[:, halves[h]], in_=grouped[h][:]
-                )
-
-            interleave(nc.scalar.copy, 1, HALF // 2, HALF)
-            interleave(nc.vector.tensor_copy, 0, 0, HALF)
-            interleave(nc.vector.tensor_copy, 1, 0, HALF // 2)
-            quantize(0)
-            quantize(1)
+            for n, cols in enumerate(thirds):
+                nc.vector.quantize_mx(out=codes[:, cols].bitcast(FP8X4), scales=scales[:, cols], in_=grouped[n][:])
             return codes, scales
 
         for q in range(4):
             nc.vector.tensor_copy(scale_table[32 * q : 32 * q + 4, :].bitcast(I32), scale_rows[32 * q : 32 * q + 4, :])
         xq_scales = sb("xq_scales", [P, S], U8)
-        xc_scales_listed = sb("xc_scales_listed", [P, S], U8)
         xc_scales = sb("xc_scales", [P, S], U8)
         nc.vector.tensor_copy(xq_scales[:], scale_table[:].indirect(offs_sb[:]))
-        nc.vector.tensor_copy(xc_scales_listed[:], scale_table[:].indirect(cand_sb[:]))
-        nc.vector.tensor_copy(
-            out=xc_scales[:].rearrange("p (t c i) -> p c t i", t=PACK, i=16),
-            in_=xc_scales_listed[:].rearrange("p (c i t) -> p c t i", t=PACK, i=16),
-        )
 
         w1_grouped = sb("w1_grouped", [P, PACK * S], BF16, tag="residual")
-        for h in range(2):
-            nc.scalar.copy(
-                out=w1_grouped[:].rearrange("p (t m j) -> p m j t", t=PACK, j=PACK)[:, h * P // 2 : (h + 1) * P // 2],
-                in_=w1_raw[h][:].rearrange("p j (m t) -> p m j t", t=PACK),
+        for h, copy in enumerate((nc.scalar.copy, nc.vector.tensor_copy)):
+            copy(
+                w1_grouped[:].rearrange("p (t m j) -> p m j t", t=PACK, j=PACK)[:, h * P // 2 : (h + 1) * P // 2],
+                w1_raw[:, :, halves[h]].rearrange("p j (m t) -> p m j t", t=PACK),
             )
         w1_codes = sb("w1_codes", [P, S], U32)
-        w1_scales = sb("w1_scales", [P, S], U8, tag="xc_scales_listed")
+        w1_scales = sb("w1_scales", [P, S], U8)
         nc.vector.quantize_mx(out=w1_codes[:].bitcast(FP8X4), scales=w1_scales[:], in_=w1_grouped[:])
 
-        xq_words = sb("xq_words", [P, S], U32, tag="scale_table")
+        xq_words = sb("xq_words", [P, S], U32)
         xc_words_listed = sb("xc_words_listed", [P, S], U32)
         xc_words = sb("xc_words", [P, S], U32)
         for h in range(2):
@@ -137,26 +125,25 @@ def tile_picked_readtwicpbig_none_p_kernel(
             out=xc_words[:].rearrange("p (t c i) -> p c t i", t=PACK, i=4),
             in_=xc_words_listed[:].rearrange("p (c i t) -> p c t i", t=PACK, i=4),
         )
+        xc_scales_listed = sb("xc_scales_listed", [P, S], U8, tag="word_table")
+        nc.vector.tensor_copy(xc_scales_listed[:], scale_table[:].indirect(cand_sb[:]))
+        nc.vector.tensor_copy(
+            out=xc_scales[:].rearrange("p (t c i) -> p c t i", t=PACK, i=16),
+            in_=xc_scales_listed[:].rearrange("p (c i t) -> p c t i", t=PACK, i=16),
+        )
 
-        w2_raw = [sb("w2_raw%d" % h, [P, PACK, HALF], F32, tag="weights%d" % h) for h in range(2)]
+        w2_raw = sb("w2_raw", [P, PACK, S], F32, tag="weights")
         res_sb = sb("res_sb", [P, PACK, S], F32, tag="residual")
-        for h in range(2):
-            nc.sync.dma_start(out=w2_raw[h][:], in_=w2.rearrange("(p j) c -> p j c", j=PACK)[:, :, halves[h]])
+        nc.sync.dma_start(out=w2_raw[:], in_=w2.rearrange("(p j) c -> p j c", j=PACK))
         nc.sync.dma_start(out=res_sb[:], in_=res.rearrange("(t p) c -> p t c", p=P))
 
         fetched = [sb("fetched%d" % t, [P, S], F32) for t in range(PACK)]
         larger = [sb("larger%d" % t, [P, S], F32) for t in range(PACK)]
 
-        def weigh(planes, t, weight):
-            if t < PACK - 1:
-                nc.scalar.activation(planes[:, t, :], larger[t][:], ACT.Copy, scale=weight[:, t : t + 1])
-            else:
-                nc.vector.tensor_scalar(planes[:, t, :], larger[t][:], weight[:, t : t + 1], None, ALU.mult)
-
-        def row_products(name, lhs, rhs):
+        def row_products(name, lhs, rhs, first_cols):
             pieces = []
             for t in range(PACK):
-                for cols in halves if t == 0 else [slice(0, S)]:
+                for cols in first_cols if t == 0 else [slice(0, S)]:
                     acc = bank("%s%d" % (name, len(pieces)), len(pieces), [P, cols.stop - cols.start])
                     product(acc[:], lhs, rhs, t, cols)
                     pieces.append((t, cols, acc))
@@ -169,7 +156,7 @@ def tile_picked_readtwicpbig_none_p_kernel(
             return slice(cols.start // 16, cols.stop // 16)
 
         z_planes = sb("z_planes", [P, PACK, S], BF16)
-        y_pieces = row_products("y", (w1_codes, w1_scales), (xq_words, xq_scales))
+        y_pieces = row_products("y", (w1_codes, w1_scales), (xq_words, xq_scales), halves)
         for t in range(PACK):
             for row, cols, acc in [piece for piece in y_pieces if piece[0] == t]:
                 nc.scalar.copy(y_rows[t % 2][:, cols], acc[:])
@@ -180,35 +167,78 @@ def tile_picked_readtwicpbig_none_p_kernel(
             for row, cols, acc in [piece for piece in y_pieces if piece[0] == t]:
                 nc.vector.tensor_tensor(gated[t][:, cols], acc[:], gated[t][:, shifted(cols)], ALU.mult)
 
+        last = PACK - 1
         gate(0)
-        for t in range(PACK):
+        for t in range(last):
             nc.vector.tensor_copy(fetched[t][:], gated[t][:].indirect(n1_sb[:]))
-            if t + 1 < PACK:
-                gate(t + 1)
+            gate(t + 1)
             nc.vector.tensor_tensor(larger[t][:], gated[t][:, :S], fetched[t][:], ALU.max)
-            weigh(z_planes, t, gs_sb)
-        z_q = interleave_and_quantize("z", z_planes)
-
+            nc.scalar.activation(z_planes[:, t, :], larger[t][:], ACT.Copy, scale=gs_sb[:, t : t + 1])
+        for cols in halves:
+            nc.vector.tensor_copy(fetched[last][:, cols], gated[last][:].indirect(n1_sb[:, listed(cols)]))
+        for cols in halves:
+            nc.vector.tensor_tensor(larger[last][:, cols], gated[last][:, cols], fetched[last][:, cols], ALU.max)
+        nc.vector.tensor_scalar(
+            z_planes[:, last, halves[0]], larger[last][:, halves[0]], gs_sb[:, last:], None, ALU.mult
+        )
+        nc.scalar.activation(z_planes[:, last, halves[1]], larger[last][:, halves[1]], ACT.Copy, scale=gs_sb[:, last:])
         w2_grouped = sb("w2_grouped", [P, PACK * S], BF16, tag="y_row1")
         for h in range(2):
             nc.scalar.copy(
                 out=w2_grouped[:, h * PACK * HALF : (h + 1) * PACK * HALF].rearrange("p (c i j) -> p c j i", i=4, j=PACK),
-                in_=w2_raw[h][:].rearrange("p j (c i) -> p c j i", i=4),
+                in_=w2_raw[:, :, halves[h]].rearrange("p j (c i) -> p c j i", i=4),
             )
-        w2_codes = sb("w2_codes", [P, S], U32, tag="z_grouped1")
+        z_q = interleave_and_quantize("z", z_planes, ("grouped0", "grouped1", "weights"))
+
+        w2_codes = sb("w2_codes", [P, S], U32, tag="weights")
         w2_scales = sb("w2_scales", [P, S], U8)
         nc.vector.quantize_mx(out=w2_codes[:].bitcast(FP8X4), scales=w2_scales[:], in_=w2_grouped[:])
 
         z2_planes = sb("z2_planes", [P, PACK, S], BF16)
-        for t, cols, acc in row_products("s", (xc_words, xc_scales), z_q):
-            nc.scalar.activation(gated[t][:, cols], acc[:], ACT.Copy, scale=0.0625)
-        nc.vector.tensor_copy(fetched[0][:], gated[0][:].indirect(n2_sb[:]))
-        for t in range(PACK):
-            if t + 1 < PACK:
-                nc.vector.tensor_copy(fetched[t + 1][:], gated[t + 1][:].indirect(n2_sb[:]))
-            nc.vector.tensor_tensor(larger[t][:], gated[t][:, :S], fetched[t][:], ALU.max)
-            weigh(z2_planes, t, gt_sb)
-        z2_q = interleave_and_quantize("z2", z2_planes)
+        gt_size = sb("gt_size", [P, PACK], F32)
+        gt_sign = sb("gt_sign", [P, PACK], F32)
+        nc.scalar.activation(gt_size[:], gt_sb[:], ACT.Abs, scale=0.0625)
+        nc.scalar.activation(gt_sign[:], gt_sb[:], ACT.Sign)
+        own = [sb("own%d" % t, [P, S], BF16) for t in range(PACK)]
+        other = [sb("other%d" % u, [P, S], BF16) for u in range(2)]
+        best = [sb("best%d" % t, [P, S], BF16) for t in range(PACK)]
+        s_pieces = row_products("s", (xc_words, xc_scales), z_q, thirds)
+
+        def scaled_copy(dst, t):
+            for row, cols, acc in [piece for piece in s_pieces if piece[0] == t]:
+                nc.scalar.activation(dst[:, cols], acc[:], ACT.Copy, scale=gt_size[:, t : t + 1])
+
+        def fetch(t, cols):
+            nc.vector.tensor_copy(other[t % 2][:, cols], gated[t][:].indirect(n2_sb[:, listed(cols)]))
+
+        def choose(t, cols):
+            nc.vector.tensor_tensor(best[t][:, cols], own[t][:, cols], other[t % 2][:, cols], ALU.max)
+
+        def sign(t, cols):
+            nc.scalar.activation(z2_planes[:, t, cols], best[t][:, cols], ACT.Copy, scale=gt_sign[:, t : t + 1])
+
+        whole = slice(0, S)
+        scaled_copy(gated[0], 0)
+        scaled_copy(gated[1], 1)
+        nc.scalar.copy(own[0][:], gated[0][:, :S])
+        fetch(0, whole)
+        for t in range(last):
+            if t + 2 < PACK:
+                scaled_copy(gated[t + 2], t + 2)
+            if t > 0:
+                sign(t - 1, whole)
+            nc.scalar.copy(own[t + 1][:], gated[t + 1][:, :S])
+            for cols in halves if t + 1 == last else [whole]:
+                fetch(t + 1, cols)
+            choose(t, whole)
+        sign(last - 1, whole)
+        for cols in halves:
+            choose(last, cols)
+        nc.vector.tensor_scalar(
+            z2_planes[:, last, halves[0]], best[last][:, halves[0]], gt_sign[:, last:], None, ALU.mult
+        )
+        sign(last, halves[1])
+        z2_q = interleave_and_quantize("z2", z2_planes, ("grouped0", "grouped1", "grouped2"))
 
         out_rows = out.rearrange("(t p) c -> p t c", p=P)
         for h in range(2):

from contextlib import ExitStack

import concourse.mybir as mybir

K, T, S = 512, 2048, 512
P = 128
PACK = 4
HALF = S // 2
FLOPS = 3 * 2 * 512 * 512 * 512

F32 = mybir.dt.float32
BF16 = mybir.dt.bfloat16
I32 = mybir.dt.int32
U32 = mybir.dt.uint32
U16 = mybir.dt.uint16
U8 = mybir.dt.uint8
FP8X4 = mybir.dt.float8_e4m3fn_x4
ALU = mybir.AluOpType
ACT = mybir.ActivationFunctionType


def tile_picked_readtwicpbig_none_p_kernel(
    tc, x_words, x_scales, w1, gs, res, gt, w2, offs, n1, cand, n2, out
):
    nc = tc.nc
    with ExitStack() as ctx:
        keep = ctx.enter_context(tc.tile_pool(name="keep", bufs=1))
        psum = ctx.enter_context(tc.psum_pool(name="psum", bufs=1))

        def sb(name, shape, dtype, tag=None):
            return keep.tile(shape, dtype, name=name, tag=tag or name, align_bytes=64)

        def bank(name, number, shape):
            return psum.tile(shape, F32, name=name, tag="bank%d" % number)

        halves = [slice(h * HALF, (h + 1) * HALF) for h in range(2)]
        thirds = [halves[0], slice(HALF, HALF + P), slice(HALF + P, S)]
        list_halves = [slice(h * HALF // 16, (h + 1) * HALF // 16) for h in range(2)]

        offs_sb = keep.tile([P, S // 16], U16, name="offs_sb")
        cand_sb = keep.tile([P, S // 16], U16, name="cand_sb")
        n1_sb = keep.tile([P, S // 16], U16, name="n1_sb")
        n2_sb = keep.tile([P, S // 16], U16, name="n2_sb")

        scale_table = sb("scale_table", [P, T], U8)
        word_table = sb("word_table", [P, T], U32)
        w1_raw = sb("w1_raw", [P, PACK, S], F32, tag="weights")
        gs_sb = sb("gs_sb", [P, PACK], F32)
        gt_sb = sb("gt_sb", [P, PACK], F32)
        y_rows = [sb("y_row%d" % u, [P, 2 * S], F32) for u in range(2)]
        gated = [sb("gated%d" % t, [P, 2 * S], F32) for t in range(PACK)]

        scale_rows = sb("scale_rows", [P, T // 4], I32)
        for q in range(4):
            nc.sync.dma_start(
                out=scale_rows[32 * q : 32 * q + 4, :], in_=x_scales[0, 4 * q : 4 * q + 4, :].bitcast(I32)
            )
        nc.sync.dma_start(offs_sb[:], offs)
        nc.sync.dma_start(out=w1_raw[:], in_=w1.rearrange("(p j) c -> p j c", j=PACK))
        nc.sync.dma_start(out=word_table[:].bitcast(I32), in_=x_words[0].rearrange("p c r -> p (c r)").bitcast(I32))
        nc.sync.dma_start(cand_sb[:], cand)
        nc.sync.dma_start(n1_sb[:], n1)
        nc.sync.dma_start(out=gs_sb[:], in_=gs.rearrange("(p t) o -> p (t o)", t=PACK))
        nc.sync.dma_start(n2_sb[:], n2)
        nc.sync.dma_start(out=gt_sb[:], in_=gt.rearrange("(p t) o -> p (t o)", t=PACK))
        nc.vector.memset(scale_table[:].bitcast(I32), 0)
        for u in range(2):
            nc.vector.memset(y_rows[u][:, S:].bitcast(I32), 0)


        warm = sb("warm", [P, 1], F32)
        nc.scalar.activation(warm[:], y_rows[0][:, S : S + 1], ACT.Sigmoid)

        def product(acc, lhs, rhs, t, cols):
            lhs_cols = slice(t * P, (t + 1) * P)
            nc.tensor.matmul_mx(
                out=acc,
                lhsT=lhs[0][:, lhs_cols].bitcast(FP8X4),
                lhsT_scale=lhs[1][:, lhs_cols],
                rhs=rhs[0][:, cols].bitcast(FP8X4),
                rhs_scale=rhs[1][:, cols],
                start=True,
                stop=True,
            )

        def interleave_and_quantize(name, planes, tags):
            codes = sb(name + "_codes", [P, S], U32)
            scales = sb(name + "_scales", [P, S], U8)
            grouped = [
                sb("%s_grouped%d" % (name, n), [P, PACK * (cols.stop - cols.start)], BF16, tag=tags[n])
                for n, cols in enumerate(thirds)
            ]
            for n, copy in enumerate((nc.vector.tensor_copy, nc.vector.tensor_copy, nc.scalar.copy)):
                copy(
                    grouped[n][:].rearrange("p (c i t) -> p c t i", i=4, t=PACK),
                    planes[:, :, thirds[n]].rearrange("p t (c i) -> p c t i", i=4),
                )
            for n, cols in enumerate(thirds):
                nc.vector.quantize_mx(out=codes[:, cols].bitcast(FP8X4), scales=scales[:, cols], in_=grouped[n][:])
            return codes, scales

        for q in range(4):
            nc.vector.tensor_copy(scale_table[32 * q : 32 * q + 4, :].bitcast(I32), scale_rows[32 * q : 32 * q + 4, :])
        xq_scales = sb("xq_scales", [P, S], U8)
        xc_scales = sb("xc_scales", [P, S], U8)
        nc.vector.tensor_copy(xq_scales[:], scale_table[:].indirect(offs_sb[:]))

        w1_grouped = sb("w1_grouped", [P, PACK * S], BF16, tag="residual")
        for h, copy in enumerate((nc.scalar.copy, nc.vector.tensor_copy)):
            copy(
                w1_grouped[:].rearrange("p (t m j) -> p m j t", t=PACK, j=PACK)[:, h * P // 2 : (h + 1) * P // 2],
                w1_raw[:, :, halves[h]].rearrange("p j (m t) -> p m j t", t=PACK),
            )
        w1_codes = sb("w1_codes", [P, S], U32)
        w1_scales = sb("w1_scales", [P, S], U8)
        nc.vector.quantize_mx(out=w1_codes[:].bitcast(FP8X4), scales=w1_scales[:], in_=w1_grouped[:])

        xq_words = sb("xq_words", [P, S], U32)
        xc_words_listed = sb("xc_words_listed", [P, S], U32)
        xc_words = sb("xc_words", [P, S], U32)
        for h in range(2):
            nc.vector.tensor_copy(xq_words[:, halves[h]], word_table[:].indirect(offs_sb[:, list_halves[h]]))
        nc.vector.tensor_copy(xc_words_listed[:], word_table[:].indirect(cand_sb[:]))
        nc.vector.tensor_copy(
            out=xc_words[:].rearrange("p (t c i) -> p c t i", t=PACK, i=4),
            in_=xc_words_listed[:].rearrange("p (c i t) -> p c t i", t=PACK, i=4),
        )
        xc_scales_listed = sb("xc_scales_listed", [P, S], U8, tag="word_table")
        nc.vector.tensor_copy(xc_scales_listed[:], scale_table[:].indirect(cand_sb[:]))
        nc.vector.tensor_copy(
            out=xc_scales[:].rearrange("p (t c i) -> p c t i", t=PACK, i=16),
            in_=xc_scales_listed[:].rearrange("p (c i t) -> p c t i", t=PACK, i=16),
        )

        w2_raw = sb("w2_raw", [P, PACK, S], F32, tag="weights")
        res_sb = sb("res_sb", [P, PACK, S], F32, tag="residual")
        nc.sync.dma_start(out=w2_raw[:], in_=w2.rearrange("(p j) c -> p j c", j=PACK))
        nc.sync.dma_start(out=res_sb[:], in_=res.rearrange("(t p) c -> p t c", p=P))

        fetched = [sb("fetched%d" % t, [P, S], F32) for t in range(PACK)]
        larger = [sb("larger%d" % t, [P, S], F32) for t in range(PACK)]

        def row_products(name, lhs, rhs, first_cols):
            pieces = []
            for t in range(PACK):
                for cols in first_cols if t == 0 else [slice(0, S)]:
                    acc = bank("%s%d" % (name, len(pieces)), len(pieces), [P, cols.stop - cols.start])
                    product(acc[:], lhs, rhs, t, cols)
                    pieces.append((t, cols, acc))
            return pieces

        def shifted(cols):
            return slice(cols.start + S, cols.stop + S)

        def listed(cols):
            return slice(cols.start // 16, cols.stop // 16)

        z_planes = sb("z_planes", [P, PACK, S], BF16)
        y_pieces = row_products("y", (w1_codes, w1_scales), (xq_words, xq_scales), halves)
        for t in range(PACK):
            for row, cols, acc in [piece for piece in y_pieces if piece[0] == t]:
                nc.scalar.copy(y_rows[t % 2][:, cols], acc[:])
            for row, cols, acc in [piece for piece in y_pieces if piece[0] == t]:
                nc.scalar.activation(gated[t][:, shifted(cols)], y_rows[t % 2][:].indirect(n1_sb[:, listed(cols)]), ACT.Sigmoid)

        def gate(t):
            for row, cols, acc in [piece for piece in y_pieces if piece[0] == t]:
                nc.vector.tensor_tensor(gated[t][:, cols], acc[:], gated[t][:, shifted(cols)], ALU.mult)

        last = PACK - 1
        gate(0)
        for t in range(last):
            nc.vector.tensor_copy(fetched[t][:], gated[t][:].indirect(n1_sb[:]))
            gate(t + 1)
            nc.vector.tensor_tensor(larger[t][:], gated[t][:, :S], fetched[t][:], ALU.max)
            nc.scalar.activation(z_planes[:, t, :], larger[t][:], ACT.Copy, scale=gs_sb[:, t : t + 1])
        for cols in halves:
            nc.vector.tensor_copy(fetched[last][:, cols], gated[last][:].indirect(n1_sb[:, listed(cols)]))
        for cols in halves:
            nc.vector.tensor_tensor(larger[last][:, cols], gated[last][:, cols], fetched[last][:, cols], ALU.max)
        nc.vector.tensor_scalar(
            z_planes[:, last, halves[0]], larger[last][:, halves[0]], gs_sb[:, last:], None, ALU.mult
        )
        nc.scalar.activation(z_planes[:, last, halves[1]], larger[last][:, halves[1]], ACT.Copy, scale=gs_sb[:, last:])
        w2_grouped = sb("w2_grouped", [P, PACK * S], BF16, tag="y_row1")
        for h in range(2):
            nc.scalar.copy(
                out=w2_grouped[:, h * PACK * HALF : (h + 1) * PACK * HALF].rearrange("p (c i j) -> p c j i", i=4, j=PACK),
                in_=w2_raw[:, :, halves[h]].rearrange("p j (c i) -> p c j i", i=4),
            )
        z_q = interleave_and_quantize("z", z_planes, ("grouped0", "grouped1", "weights"))

        w2_codes = sb("w2_codes", [P, S], U32, tag="weights")
        w2_scales = sb("w2_scales", [P, S], U8)
        nc.vector.quantize_mx(out=w2_codes[:].bitcast(FP8X4), scales=w2_scales[:], in_=w2_grouped[:])

        z2_planes = sb("z2_planes", [P, PACK, S], BF16)
        gt_size = sb("gt_size", [P, PACK], F32)
        gt_sign = sb("gt_sign", [P, PACK], F32)
        nc.scalar.activation(gt_size[:], gt_sb[:], ACT.Abs, scale=0.0625)
        nc.scalar.activation(gt_sign[:], gt_sb[:], ACT.Sign)
        own = [sb("own%d" % t, [P, S], BF16) for t in range(PACK)]
        other = [sb("other%d" % u, [P, S], BF16) for u in range(2)]
        best = [sb("best%d" % t, [P, S], BF16) for t in range(PACK)]
        s_pieces = row_products("s", (xc_words, xc_scales), z_q, thirds)

        def scaled_copy(dst, t):
            for row, cols, acc in [piece for piece in s_pieces if piece[0] == t]:
                nc.scalar.activation(dst[:, cols], acc[:], ACT.Copy, scale=gt_size[:, t : t + 1])

        def fetch(t, cols):
            nc.vector.tensor_copy(other[t % 2][:, cols], gated[t][:].indirect(n2_sb[:, listed(cols)]))

        def choose(t, cols):
            nc.vector.tensor_tensor(best[t][:, cols], own[t][:, cols], other[t % 2][:, cols], ALU.max)

        def sign(t, cols):
            nc.scalar.activation(z2_planes[:, t, cols], best[t][:, cols], ACT.Copy, scale=gt_sign[:, t : t + 1])

        whole = slice(0, S)
        scaled_copy(gated[0], 0)
        scaled_copy(gated[1], 1)
        nc.scalar.copy(own[0][:], gated[0][:, :S])
        fetch(0, whole)
        for t in range(last):
            if t + 2 < PACK:
                scaled_copy(gated[t + 2], t + 2)
            if t > 0:
                sign(t - 1, whole)
            nc.scalar.copy(own[t + 1][:], gated[t + 1][:, :S])
            for cols in halves if t + 1 == last else [whole]:
                fetch(t + 1, cols)
            choose(t, whole)
        sign(last - 1, whole)
        for cols in halves:
            choose(last, cols)
        nc.vector.tensor_scalar(
            z2_planes[:, last, halves[0]], best[last][:, halves[0]], gt_sign[:, last:], None, ALU.mult
        )
        sign(last, halves[1])
        z2_q = interleave_and_quantize("z2", z2_planes, ("grouped0", "grouped1", "grouped2"))

        out_rows = out.rearrange("(t p) c -> p t c", p=P)
        for h in range(2):
            for pair in range(2):
                acc = bank("o%d%d" % (h, pair), 2 * h + pair, [P, 2, HALF])
                for u in range(2):
                    product(acc[:, u, :], (w2_codes, w2_scales), z2_q, 2 * pair + u, halves[h])
                tiles = slice(2 * pair, 2 * pair + 2)
                result = sb("result%d%d" % (h, pair), [P, 2, HALF], F32)
                nc.vector.tensor_tensor(result[:], acc[:], res_sb[:, tiles, halves[h]], ALU.add)
                nc.sync.dma_start(out=out_rows[:, tiles, halves[h]], in_=result[:])
